import numpy as np
import ml_dtypes


def mxq(x, axis, fmt="e4m3"):
    dtype, down = {"e4m3": (ml_dtypes.float8_e4m3fn, 7), "e5m2": (ml_dtypes.float8_e5m2, 14)}[fmt]
    v = np.moveaxis(np.asarray(x, np.float32).astype(ml_dtypes.bfloat16).astype(np.float64), axis, -1)
    blocks = v.reshape(v.shape[:-1] + (-1, 32))
    amax = np.abs(blocks).max(-1, keepdims=True)
    byte = np.maximum(np.where(amax > 0, np.frexp(amax)[1] - 1 + 127, 0) - down, 1)
    scale = np.exp2(byte - 127.0)
    codes = (blocks / scale).astype(np.float32).astype(dtype).astype(np.float64)
    return np.moveaxis((codes * scale).reshape(v.shape), -1, axis)


WIDE = False


def mx_kscale(k):
    if not WIDE:
        return np.ones(k)
    levels = np.array([10, -10, 5, -5, 0])
    if k % 512:
        return np.exp2(np.random.permutation(np.resize(levels, k // 32))).repeat(32)
    a = np.empty((k // 512, 16))
    for p in range(k // 512):
        a[p, :8] = np.random.permutation(np.resize(levels, 8))
        for g in range(8):
            far = levels[np.abs(levels - a[p, g]) >= 10]
            a[p, g + 8] = far[np.random.randint(len(far))]
    return np.exp2(a.ravel()).repeat(32)


BF16 = ml_dtypes.bfloat16


def bf(x):
    return np.asarray(x, np.float32).astype(BF16)


def f64(x):
    return np.asarray(x).astype(np.float64)


E2M1 = np.array([0.0, 0.5, 1.0, 1.5, 2.0, 3.0, 4.0, 6.0, -0.0, -0.5, -1.0, -1.5, -2.0, -3.0, -4.0, -6.0])


def pack_weight(w, fmt):
    k, n = w.shape
    w = f64(bf(w)).reshape(k // 32, 32, n)
    amax = np.abs(w).max(1)
    if fmt == "e4m3":
        byte = np.frexp(amax)[1] - 1 + 127 - 7
    else:
        mant, ex = np.frexp(amax / 6.0)
        byte = np.where(mant > 0.5, ex, ex - 1) + 127
    byte = np.clip(np.where(amax > 0, byte, 1), 1, 254)
    scaled = (w * np.exp2(127.0 - byte)[:, None, :]).reshape(k, n).astype(np.float32)
    by_word = np.ascontiguousarray(scaled.reshape(k // 512, 128, 4, n).transpose(0, 1, 3, 2))
    if fmt == "e4m3":
        words = by_word.astype(ml_dtypes.float8_e4m3fn).view(np.uint8)
    else:
        c = by_word.astype(ml_dtypes.float4_e2m1fn).view(np.uint8) & 0xF
        words = c[..., 0::2] | (c[..., 1::2] << 4)
    return np.ascontiguousarray(words), np.ascontiguousarray(byte.astype(np.uint8).reshape(k // 512, 16, n))


def unpack_weight(words, scales, fmt):
    g, p, n, _ = words.shape
    if fmt == "e4m3":
        vals = np.ascontiguousarray(words).view(ml_dtypes.float8_e4m3fn).astype(np.float64)
    else:
        nib = np.empty((g, p, n, 4), np.uint8)
        nib[..., 0::2] = words & 0xF
        nib[..., 1::2] = words >> 4
        vals = E2M1[nib]
    vals = vals * np.repeat(np.exp2(scales.astype(np.float64) - 127.0), 8, axis=1)[..., None]
    return vals.transpose(0, 1, 3, 2).reshape(g * 512, n)
def pack4(w):
    words, scales = pack_weight(w, "e2m1")
    return words.reshape(words.shape[0], 128, -1), scales


def unpack4(words, scales):
    return unpack_weight(words.reshape(words.shape[0], 128, -1, 2), scales, "e2m1")


def planes(Y):
    n, m = Y.shape
    b = f64(bf(Y)).reshape(n // 32, 32, m)
    amax = np.abs(b).max(1)
    byte = np.clip(np.where(amax > 0, np.frexp(amax)[1] - 1 + 127 - 7, 1), 1, 254)
    codes = (b * np.exp2(127.0 - byte)[:, None, :]).reshape(n, m).astype(np.float32).astype(ml_dtypes.float8_e4m3fn).view(np.uint8)
    words = codes.reshape(n // 512, 128, 4, m).transpose(0, 1, 3, 2)
    return np.ascontiguousarray(words), np.ascontiguousarray(byte.astype(np.uint8).reshape(n // 512, 16, m))


P, C, N1, N2, D, F = 4, 256, 1024, 1024, 1024, 1024

def soft_assignments(n):
    logits = 2.0 * np.random.randn(P, n, C)
    e = np.exp(logits - logits.max(axis=2, keepdims=True))
    return e / e.sum(axis=2, keepdims=True)

def setup_inputs():
    s1, s2, t = mx_kscale(N1), mx_kscale(N2), mx_kscale(D)
    a_live, a_arch = soft_assignments(N1), soft_assignments(N2)
    mass = a_live.sum(axis=1) + a_arch.sum(axis=1)
    x_live = np.random.randn(P, N1, D) / s1[:, None] * t
    arch = np.random.randn(P, N2, D) / s2[:, None] * t
    arch_words, arch_scales = pack4(arch.transpose(1, 0, 2).reshape(N2, P * D))
    centres = 1.2 * C / (N1 + N2) * np.random.randn(C, D) * t
    spread = np.exp(0.8 * np.random.randn(F))
    w_proj = np.random.randn(D, F) / np.sqrt(D) * spread / t[:, None]
    return {"a_live": bf(a_live * s1[:, None]), "x_live": bf(x_live),
            "a_arch": bf(a_arch * s2[:, None]), "arch_words": arch_words, "arch_scales": arch_scales,
            "mass": bf(mass), "centres": bf(centres), "w_proj": bf(w_proj)}

def reference(a_live, x_live, a_arch, arch_words, arch_scales, mass, centres, w_proj):
    al = mxq(f64(a_live), 1, "e4m3")
    xl = mxq(f64(x_live), 1, "e4m3")
    aa = mxq(f64(a_arch), 1, "e4m3")
    xa = unpack4(arch_words, arch_scales).reshape(N2, P, D).transpose(1, 0, 2)
    total = (al.transpose(0, 2, 1) @ xl) + (aa.transpose(0, 2, 1) @ xa)
    v = (total - f64(mass)[:, :, None] * f64(centres)).reshape(P * C, D)
    z = mxq(v, 1, "e4m3") @ mxq(f64(w_proj), 0, "e4m3")
    y = (z * (1.0 + np.abs(z)) ** -0.5).reshape(P, C, F)
    Y = y.reshape(P * C, F).T
    words, scales = planes(Y)
    return y, words, scales

@@ -1,0 +1,463 @@
+from contextlib import ExitStack
+
+import concourse.mybir as mybir
+from concourse.masks import make_identity
+
+PLACES, CLUSTERS, DESCR, WIDTH, PROJ = 4, 256, 1024, 1024, 1024
+FLOPS = 2 * PLACES * CLUSTERS * WIDTH * 2 * DESCR + 2 * PLACES * CLUSTERS * WIDTH * PROJ
+
+F32 = mybir.dt.float32
+BF16 = mybir.dt.bfloat16
+U32 = mybir.dt.uint32
+I32 = mybir.dt.int32
+U8 = mybir.dt.uint8
+FP8X4 = mybir.dt.float8_e4m3fn_x4
+FP4X4 = mybir.dt.float4_e2m1fn_x4
+ALU = mybir.AluOpType
+ACT = mybir.ActivationFunctionType
+
+P = 128
+PACK = 4
+BANK = 512
+GROUPS = 2
+UNITS = 2 * PLACES
+VECTOR_COLUMNS = 256
+EARLY_UNITS = 4
+
+
+def tile_vlad_two_source_projection_k6_kernel(
+    tc, a_live, x_live, a_arch, arch_words, arch_scales, mass, centres, w_proj, out_0, out_1, out_2
+):
+    nc = tc.nc
+    with ExitStack() as ctx:
+        keep = ctx.enter_context(tc.tile_pool(name="keep", bufs=1))
+        flow = ctx.enter_context(tc.tile_pool(name="flow", bufs=2))
+        psum = ctx.enter_context(tc.psum_pool(name="psum", bufs=1))
+        ctx.enter_context(tc.manual_schedule())
+
+        ident = keep.tile([P, P], F32, name="ident")
+        make_identity(nc, ident[:])
+        arch_planes = []
+        for place in range(PLACES):
+            plane = keep.tile([P, GROUPS, WIDTH], U8, name="arch_plane_%d" % place, align_bytes=64)
+            nc.vector.memset(plane[:].bitcast(I32), 0)
+            arch_planes.append(plane)
+
+        def load_arch_scales(place):
+            cols = slice(place * WIDTH, (place + 1) * WIDTH)
+            for quad in range(4):
+                nc.sync.dma_start(
+                    out=arch_planes[place][32 * quad : 32 * quad + 4, :, :].bitcast(I32),
+                    in_=arch_scales[:, 4 * quad : 4 * quad + 4, cols].rearrange("g r n -> r g n").bitcast(I32),
+                )
+
+        raw_a, raw_x, arch = {}, {}, {}
+
+        def load_assignments(key, source, pieces):
+            tile = flow.tile([P, GROUPS, PACK, CLUSTERS], BF16, name="raw_a", tag="raw_a", bufs=4)
+            rows = source.rearrange("(g p j) c -> p g j c", g=GROUPS, j=PACK)
+            step = GROUPS // pieces
+            for g in range(0, GROUPS, step):
+                nc.sync.dma_start(out=tile[:, g : g + step], in_=rows[:, g : g + step])
+            raw_a[key] = tile
+
+        def load_rows(key, source, g, pieces=1):
+            tile = flow.tile([P, PACK, WIDTH], BF16, name="raw_x", tag="raw_x", bufs=6)
+            rows = source[g * BANK : (g + 1) * BANK, :].rearrange("(p j) d -> p j d", j=PACK)
+            step = WIDTH // pieces
+            for at in range(0, WIDTH, step):
+                nc.sync.dma_start(out=tile[:, :, at : at + step], in_=rows[:, :, at : at + step])
+            raw_x[key, g] = tile
+
+        def load_arch(place):
+            tile = flow.tile([P, GROUPS, 2 * WIDTH], U8, name="arch", tag="arch", bufs=PLACES, align_bytes=64)
+            window = arch_words.rearrange("g p b -> p g b")[:, :, 2 * WIDTH * place : 2 * WIDTH * (place + 1)]
+            nc.sync.dma_start(out=tile[:].bitcast(I32), in_=window.bitcast(I32))
+            arch[place] = tile
+
+        def load_place(place):
+            load_assignments(("live", place), a_live[place], 1)
+            load_rows(place, x_live[place], 0)
+            load_assignments(("arch", place), a_arch[place], 1)
+            load_rows(place, x_live[place], 1)
+            load_arch(place)
+            load_arch_scales(place)
+
+        mass_rows = keep.tile([UNITS, P], BF16, name="mass_rows")
+        load_assignments(("live", 0), a_live[0], 2)
+        load_rows(0, x_live[0], 0, 2)
+        load_assignments(("arch", 0), a_arch[0], 1)
+        load_rows(0, x_live[0], 1)
+        nc.sync.dma_start(out=mass_rows[:], in_=mass.rearrange("i (h p) -> (i h) p", p=P))
+        load_arch_scales(0)
+        load_rows("w", w_proj, 0)
+        load_arch(0)
+        centres_sb = [keep.tile([P, WIDTH], BF16, name="centres_%d" % h) for h in range(2)]
+        nc.sync.dma_start(out=centres_sb[0][:], in_=centres[0:P, :])
+        load_rows("w", w_proj, 1)
+        nc.sync.dma_start(out=centres_sb[1][:], in_=centres[P : 2 * P, :])
+        load_place(1)
+
+        mass_square = keep.tile([P, P], F32, name="mass_square")
+        minus_mass = keep.tile([P, UNITS], F32, name="minus_mass")
+
+        def spread_mass():
+            nc.scalar.activation(out=mass_square[0:UNITS, :], in_=mass_rows[:], func=ACT.Copy, scale=-1.0)
+            mass_bank = psum.tile([P, BANK], F32, name="y_turned", tag="y_turned")
+            nc.tensor.transpose(mass_bank[:, 0:P], mass_square[:], ident[:])
+            return mass_bank
+
+        nc.scalar.activation(out=mass_square[:], in_=ident[:], func=ACT.Abs_reciprocal_sqrt, bias=1.0)
+
+        grouped, quantised = {}, {}
+
+        def interleave(engine_copy, dst, src):
+            engine_copy(
+                out=dst.rearrange("p (c i) t -> p c t i", i=4),
+                in_=src.rearrange("p t (c i) -> p c t i", i=4),
+            )
+
+        def chunk_share(key, on_vector):
+            if key not in grouped:
+                grouped[key] = flow.tile([P, BANK * PACK], BF16, name="grouped", tag="grouped", bufs=4, align_bytes=64)
+            dst = grouped[key][:].rearrange("p (c t) -> p c t", t=PACK)
+            if key[0] in ("live", "arch"):
+                g = 0 if on_vector else 1
+                return dst[:, g * CLUSTERS : (g + 1) * CLUSTERS, :], raw_a[key][:, g]
+            source, g, half = key
+            cols = slice(0, VECTOR_COLUMNS) if on_vector else slice(VECTOR_COLUMNS, BANK)
+            return dst[:, cols, :], raw_x[source, g][:, :, half * BANK + cols.start : half * BANK + cols.stop]
+
+        def copy_v(key):
+            interleave(nc.vector.tensor_copy, *chunk_share(key, True))
+
+        def copy_s(key):
+            interleave(nc.scalar.copy, *chunk_share(key, False))
+
+        def quantise(key):
+            tag, bufs = ("w", 4) if key[0] == "w" else ("op", 13)
+            codes = flow.tile([P, BANK], U32, name="codes", tag=tag + "_codes", bufs=bufs, align_bytes=64)
+            scales = flow.tile([P, BANK], U8, name="scales", tag=tag + "_scales", bufs=bufs, align_bytes=64)
+            nc.vector.quantize_mx(out=codes[:].bitcast(FP8X4), scales=scales[:], in_=grouped[key][:])
+            quantised[key] = (codes, scales)
+
+        sums, v_rows, v_bank, v_cols, v_q, z, root, y, y_rows, y_bank, y_cols = ({} for k in range(11))
+
+        issued = {}
+
+        def bank(pair, half):
+            return psum.tile([P, BANK], F32, name="bank", tag="bank%d" % (2 * pair + half))
+
+        def sum_pass(unit, half, source, g):
+            place, h = divmod(unit, 2)
+            issued[unit, half] = issued.get((unit, half), 0) + 1
+            start, stop = issued[unit, half] == 1, issued[unit, half] == 2 * GROUPS
+            if start:
+                sums[unit, half] = bank(unit % 2, half)
+            a_codes, a_scales = quantised[source, place]
+            cols = slice(g * CLUSTERS + h * P, g * CLUSTERS + (h + 1) * P)
+            if source == "live":
+                codes, scales = quantised[place, g, half]
+                rhs, rhs_scale = codes[:].bitcast(FP8X4), scales[:]
+            else:
+                rhs = arch[place][:, g, 2 * half * BANK : 2 * (half + 1) * BANK].bitcast(FP4X4)
+                rhs_scale = arch_planes[place][:, g, half * BANK : (half + 1) * BANK]
+            nc.tensor.matmul_mx(
+                out=sums[unit, half][:], lhsT=a_codes[:, cols].bitcast(FP8X4), lhsT_scale=a_scales[:, cols],
+                rhs=rhs, rhs_scale=rhs_scale, start=start, stop=stop,
+            )
+
+        def sum_first(unit):
+            for half in range(2):
+                sum_pass(unit, half, "live", 0)
+
+        def sum_arch(unit):
+            for half in range(2):
+                for g in range(GROUPS):
+                    sum_pass(unit, half, "arch", g)
+
+        def sum_all(unit):
+            sum_first(unit)
+            sum_arch(unit)
+            for half in range(2):
+                sum_pass(unit, half, "live", 1)
+
+        def subtract_centres(unit):
+            for half in range(2):
+                tile = flow.tile([P, BANK], BF16, name="v_rows", tag="v_rows", bufs=4)
+                nc.vector.scalar_tensor_tensor(
+                    out=tile[:], in0=centres_sb[unit % 2][:, half * BANK : (half + 1) * BANK],
+                    scalar=minus_mass[:, unit : unit + 1], in1=sums[unit, half][:], op0=ALU.mult, op1=ALU.add,
+                )
+                v_rows[unit, half] = tile
+
+        def turn(target, rows, g):
+            words = rows[:].bitcast(F32)
+            for u in range(2):
+                at = (2 * g + u) * P
+                nc.tensor.transpose(target[:, at : at + P], words[:, u : 2 * P : 2], ident[:])
+
+        def turn_v(unit, tag="v_turned"):
+            v_bank[unit] = psum.tile([P, BANK], F32, name=tag, tag=tag)
+            for g in range(GROUPS):
+                turn(v_bank[unit], v_rows[unit, g], g)
+
+        def gather_words(engine_copy, dst, source):
+            engine_copy(
+                out=dst[:].bitcast(F32).rearrange("p (g c u) -> p g c u", g=GROUPS, u=2),
+                in_=source[:].rearrange("p (g u c) -> p g c u", g=GROUPS, u=2),
+            )
+
+        def collect_v(unit, engine_copy):
+            v_cols[unit] = flow.tile([P, GROUPS * P * PACK], BF16, name="v_cols", tag="v_cols", align_bytes=64)
+            gather_words(engine_copy, v_cols[unit], v_bank[unit])
+
+        def quantise_v(unit):
+            codes = flow.tile([P, GROUPS * P], U32, name="v_codes", tag="v_codes", align_bytes=64)
+            scales = flow.tile([P, GROUPS * P], U8, name="v_scales", tag="v_scales", align_bytes=64)
+            nc.vector.quantize_mx(out=codes[:].bitcast(FP8X4), scales=scales[:], in_=v_cols[unit][:])
+            v_q[unit] = (codes, scales)
+
+        def project(unit):
+            codes, scales = v_q[unit]
+            for half in range(2):
+                z[unit, half] = bank(2 if unit < UNITS - 2 else unit % 2, half)
+                for g in range(GROUPS):
+                    w_codes, w_scales = quantised["w", g, half]
+                    cols = slice(g * P, (g + 1) * P)
+                    nc.tensor.matmul_mx(
+                        out=z[unit, half][:], lhsT=codes[:, cols].bitcast(FP8X4), lhsT_scale=scales[:, cols],
+                        rhs=w_codes[:].bitcast(FP8X4), rhs_scale=w_scales[:], start=g == 0, stop=g == GROUPS - 1,
+                    )
+
+        def inverse_root(unit):
+            size = {}
+            for half in range(2):
+                size[half] = flow.tile([P, BANK], F32, name="size", tag="size", bufs=2)
+                nc.scalar.activation(out=size[half][:], in_=z[unit, half][:], func=ACT.Abs)
+            for half in range(2):
+                root[unit, half] = flow.tile([P, BANK], F32, name="root", tag="root", bufs=4)
+                nc.scalar.activation(
+                    out=root[unit, half][:], in_=size[half][:], func=ACT.Abs_reciprocal_sqrt, bias=1.0
+                )
+
+        y_out = out_0.rearrange("i c f -> (i c) f")
+
+        def power_law(unit, between=None):
+            y[unit] = flow.tile([P, PROJ], F32, name="y", tag="y", bufs=3)
+            for half in range(2):
+                if half == 1 and between is not None:
+                    between()
+                nc.vector.tensor_tensor(
+                    out=y[unit][:, half * BANK : (half + 1) * BANK], in0=z[unit, half][:],
+                    in1=root[unit, half][:], op=ALU.mult,
+                )
+            nc.sync.dma_start(out=y_out[unit * P : (unit + 1) * P, :], in_=y[unit][:])
+
+        def round_y(unit):
+            for half in range(2):
+                y_rows[unit, half] = flow.tile([P, BANK], BF16, name="y_rows", tag="y_rows", bufs=4)
+                nc.vector.tensor_copy(out=y_rows[unit, half][:], in_=y[unit][:, half * BANK : (half + 1) * BANK])
+
+        def turn_y(unit, tag="y_turned"):
+            y_bank[unit] = psum.tile([P, BANK], F32, name=tag, tag=tag)
+            for g in range(GROUPS):
+                turn(y_bank[unit], y_rows[unit, g], g)
+
+        def collect_y(unit, engine_copy):
+            y_cols[unit] = flow.tile([P, GROUPS * P * PACK], BF16, name="y_cols", tag="y_cols", align_bytes=64)
+            gather_words(engine_copy, y_cols[unit], y_bank[unit])
+
+        early_scales = keep.tile([P, GROUPS, EARLY_UNITS * P], U8, name="early_scales", align_bytes=64)
+        late_scales = keep.tile([P, GROUPS, (UNITS - EARLY_UNITS) * P], U8, name="late_scales", align_bytes=64)
+        words_out = out_1.rearrange("g p m t -> p g (m t)").bitcast(I32)
+
+        def store_scales(queues, plane, cols):
+            for quad in range(4):
+                queues[quad % len(queues)].dma_start(
+                    out=out_2[:, 4 * quad : 4 * quad + 4, cols].rearrange("g r m -> r g m").bitcast(I32),
+                    in_=plane[32 * quad : 32 * quad + 4, :, :].bitcast(I32),
+                )
+
+        y_codes = {}
+
+        def store_words(place):
+            nc.sync.dma_start(
+                out=words_out[:, :, place * CLUSTERS : (place + 1) * CLUSTERS], in_=y_codes[place][:].bitcast(I32)
+            )
+
+        def quantise_y(unit):
+            place, h = divmod(unit, 2)
+            if h == 0:
+                y_codes[place] = flow.tile([P, GROUPS, CLUSTERS], U32, name="y_codes", tag="y_codes", align_bytes=64)
+            plane, at = (early_scales, unit * P) if unit < EARLY_UNITS else (late_scales, (unit - EARLY_UNITS) * P)
+            for g in range(GROUPS):
+                nc.vector.quantize_mx(
+                    out=y_codes[place][:, g, h * P : (h + 1) * P].bitcast(FP8X4), scales=plane[:, g, at : at + P],
+                    in_=y_cols[unit][:, g * BANK : (g + 1) * BANK],
+                )
+            if h == 1:
+                store_words(place)
+            if unit == EARLY_UNITS - 1:
+                store_scales([nc.sync], early_scales, slice(0, EARLY_UNITS * P))
+
+        def finish_last(unit):
+            y[unit] = flow.tile([P, PROJ], F32, name="y", tag="y", bufs=3)
+            at = (unit - EARLY_UNITS) * P
+            turned = {}
+
+            def rounded(half):
+                y_rows[unit, half] = flow.tile([P, BANK], BF16, name="y_rows", tag="y_rows", bufs=4)
+                nc.vector.tensor_tensor(
+                    out=y_rows[unit, half][:], in0=z[unit, half][:], in1=root[unit, half][:], op=ALU.mult
+                )
+                tag = "bank%d" % (4 + half)
+                turned[half] = psum.tile([P, BANK], F32, name=tag, tag=tag)
+                turn(turned[half], y_rows[unit, half], 0)
+
+            def exact(half):
+                window = slice(half * BANK, (half + 1) * BANK)
+                nc.vector.tensor_tensor(
+                    out=y[unit][:, window], in0=z[unit, half][:], in1=root[unit, half][:], op=ALU.mult
+                )
+                nc.sync.dma_start(out=y_out[unit * P : (unit + 1) * P, window], in_=y[unit][:, window])
+
+            def planes(half):
+                cols = flow.tile([P, P * PACK], BF16, name="last_cols", tag="last_cols", align_bytes=64)
+                nc.scalar.copy(
+                    out=cols[:].bitcast(F32).rearrange("p (c u) -> p c u", u=2),
+                    in_=turned[half][:, 0 : 2 * P].rearrange("p (u c) -> p c u", u=2),
+                )
+                nc.vector.quantize_mx(
+                    out=y_codes[unit // 2][:, half, P : 2 * P].bitcast(FP8X4), scales=late_scales[:, half, at : at + P], in_=cols[:]
+                )
+
+            return rounded, exact, planes
+
+        def place_chunks(place):
+            return [("live", place), (place, 0, 0), (place, 0, 1), ("arch", place), (place, 1, 0), (place, 1, 1)]
+
+        def feed(key, previous):
+            copy_s(key)
+            copy_v(key)
+            if previous is not None:
+                quantise(previous)
+
+        on_scalar, on_vector = nc.scalar.copy, nc.vector.tensor_copy
+
+        first = place_chunks(0)
+        stream = place_chunks(1) + place_chunks(2) + place_chunks(3)
+        w_chunks = [("w", g, half) for g in range(GROUPS) for half in range(2)]
+        feed(first[0], None)
+        feed(first[1], first[0])
+        feed(first[2], first[1])
+        feed(first[3], first[2])
+        sum_first(0)
+        sum_first(1)
+        feed(first[4], first[3])
+        mass_bank = spread_mass()
+        feed(first[5], first[4])
+        nc.scalar.copy(out=minus_mass[:], in_=mass_bank[:, 0:UNITS])
+        sum_pass(0, 0, "live", 1)
+        feed(w_chunks[0], first[5])
+        sum_pass(0, 1, "live", 1)
+        sum_pass(1, 0, "live", 1)
+        feed(w_chunks[1], w_chunks[0])
+        sum_arch(0)
+        quantise(w_chunks[1])
+        subtract_centres(0)
+        turn_v(0)
+        sum_arch(1)
+        feed(w_chunks[2], None)
+        collect_v(0, on_scalar)
+        feed(w_chunks[3], w_chunks[2])
+        quantise_v(0)
+        feed(stream[0], w_chunks[3])
+        project(0)
+        feed(stream[1], stream[0])
+        feed(stream[2], stream[1])
+        pending = stream[2]
+
+        for unit in range(1, 6):
+            chunks = stream[3 * unit : 3 * unit + 3]
+            back = unit - 2
+            if unit % 2 == 1 and unit // 2 + 2 < PLACES:
+                load_place(unit // 2 + 2)
+            if back >= 0:
+                inverse_root(back)
+            quantise(pending)
+            sum_pass(unit, 1, "live", 1)
+            sum_first(unit + 1)
+            copy_v(chunks[0])
+            copy_s(chunks[0])
+            copy_v(chunks[1])
+            copy_s(chunks[1])
+            if back > 0:
+                quantise_y(back - 1)
+            if back >= 0:
+                power_law(back)
+                project(back + 1)
+            subtract_centres(unit)
+            turn_v(unit)
+            if back >= 0:
+                round_y(back)
+                turn_y(back)
+            quantise(chunks[0])
+            sum_arch(unit + 1)
+            copy_v(chunks[2])
+            copy_s(chunks[2])
+            collect_v(unit, on_scalar)
+            if 0 <= back < 3:
+                collect_y(back, on_scalar)
+            quantise(chunks[1])
+            sum_pass(unit + 1, 0, "live", 1)
+            quantise_v(unit)
+            pending = chunks[2]
+
+        inverse_root(4)
+        sum_first(7)
+        quantise(pending)
+        sum_pass(6, 1, "live", 1)
+        sum_arch(7)
+        subtract_centres(6)
+        turn_v(6)
+        sum_pass(7, 0, "live", 1)
+        sum_pass(7, 1, "live", 1)
+        collect_y(3, on_scalar)
+        collect_v(6, on_scalar)
+        power_law(4)
+        project(5)
+        subtract_centres(7)
+        turn_v(7)
+        inverse_root(5)
+        quantise_v(6)
+        project(6)
+        round_y(4)
+        turn_y(4)
+        quantise_y(3)
+        collect_v(7, on_scalar)
+        power_law(5)
+        collect_y(4, on_vector)
+        inverse_root(6)
+        quantise_v(7)
+        project(7)
+        round_y(5)
+        turn_y(5)
+        quantise_y(4)
+        inverse_root(7)
+        power_law(6)
+        round_y(6)
+        turn_y(6, "v_turned")
+        collect_y(5, on_vector)
+        rounded, exact, planes = finish_last(7)
+        rounded(0)
+        rounded(1)
+        collect_y(6, on_scalar)
+        exact(0)
+        exact(1)
+        quantise_y(5)
+        quantise_y(6)
+        planes(0)
+        planes(1)
+        store_words(3)
+        store_scales([nc.scalar, nc.sync], late_scales, slice(EARLY_UNITS * P, UNITS * P))

@@ -21,7 +21,8 @@ PACK = 4
 BANK = 512
 GROUPS = 2
 UNITS = 2 * PLACES
-VECTOR_COLUMNS = 256
+VECTOR_NARROW = 248
+VECTOR_WIDE = 584
 EARLY_UNITS = 4
 
 
@@ -118,15 +119,20 @@ def tile_vlad_two_source_projection_k6_kernel(
             )
 
         def chunk_share(key, on_vector):
-            if key not in grouped:
-                grouped[key] = flow.tile([P, BANK * PACK], BF16, name="grouped", tag="grouped", bufs=4, align_bytes=64)
-            dst = grouped[key][:].rearrange("p (c t) -> p c t", t=PACK)
-            if key[0] in ("live", "arch"):
-                g = 0 if on_vector else 1
-                return dst[:, g * CLUSTERS : (g + 1) * CLUSTERS, :], raw_a[key][:, g]
             source, g, half = key
-            cols = slice(0, VECTOR_COLUMNS) if on_vector else slice(VECTOR_COLUMNS, BANK)
-            return dst[:, cols, :], raw_x[source, g][:, :, half * BANK + cols.start : half * BANK + cols.stop]
+            width = BANK if half is not None else 2 * BANK
+            if key not in grouped:
+                grouped[key] = flow.tile(
+                    [P, width * PACK], BF16, name="grouped", tag="grouped_%d" % width, bufs=3 if half is not None else 2, align_bytes=64
+                )
+            dst = grouped[key][:].rearrange("p (c t) -> p c t", t=PACK)
+            if source in ("live", "arch"):
+                group = 0 if on_vector else 1
+                return dst[:, group * CLUSTERS : (group + 1) * CLUSTERS, :], raw_a[source, g][:, group]
+            split = VECTOR_NARROW if half is not None else VECTOR_WIDE
+            cols = slice(0, split) if on_vector else slice(split, width)
+            at = half * BANK if half is not None else 0
+            return dst[:, cols, :], raw_x[source, g][:, :, at + cols.start : at + cols.stop]
 
         def copy_v(key):
             interleave(nc.vector.tensor_copy, *chunk_share(key, True))
@@ -135,11 +141,18 @@ def tile_vlad_two_source_projection_k6_kernel(
             interleave(nc.scalar.copy, *chunk_share(key, False))
 
         def quantise(key):
-            tag, bufs = ("w", 4) if key[0] == "w" else ("op", 13)
-            codes = flow.tile([P, BANK], U32, name="codes", tag=tag + "_codes", bufs=bufs, align_bytes=64)
-            scales = flow.tile([P, BANK], U8, name="scales", tag=tag + "_scales", bufs=bufs, align_bytes=64)
+            source, g, half = key
+            width = BANK if half is not None else 2 * BANK
+            tag, bufs = ("w", 4) if source == "w" else ("op_%d" % width, 8 if half is not None else 4)
+            codes = flow.tile([P, width], U32, name="codes", tag=tag + "_codes", bufs=bufs, align_bytes=64)
+            scales = flow.tile([P, width], U8, name="scales", tag=tag + "_scales", bufs=bufs, align_bytes=64)
             nc.vector.quantize_mx(out=codes[:].bitcast(FP8X4), scales=scales[:], in_=grouped[key][:])
-            quantised[key] = (codes, scales)
+            if half is not None:
+                quantised[key] = (codes[:], scales[:])
+            else:
+                for k in range(2):
+                    cols = slice(k * BANK, (k + 1) * BANK)
+                    quantised[source, g, k] = (codes[:, cols], scales[:, cols])
 
         sums, v_rows, v_bank, v_cols, v_q, z, root, y, y_rows, y_bank, y_cols = ({} for k in range(11))
 
@@ -154,11 +167,11 @@ def tile_vlad_two_source_projection_k6_kernel(
             start, stop = issued[unit, half] == 1, issued[unit, half] == 2 * GROUPS
             if start:
                 sums[unit, half] = bank(unit % 2, half)
-            a_codes, a_scales = quantised[source, place]
+            a_codes, a_scales = quantised[source, place, 0]
             cols = slice(g * CLUSTERS + h * P, g * CLUSTERS + (h + 1) * P)
             if source == "live":
                 codes, scales = quantised[place, g, half]
-                rhs, rhs_scale = codes[:].bitcast(FP8X4), scales[:]
+                rhs, rhs_scale = codes.bitcast(FP8X4), scales
             else:
                 rhs = arch[place][:, g, 2 * half * BANK : 2 * (half + 1) * BANK].bitcast(FP4X4)
                 rhs_scale = arch_planes[place][:, g, half * BANK : (half + 1) * BANK]
@@ -171,19 +184,17 @@ def tile_vlad_two_source_projection_k6_kernel(
             for half in range(2):
                 sum_pass(unit, half, "live", 0)
 
-        def sum_arch(unit):
-            for half in range(2):
+        def sum_arch(unit, halves=(0, 1)):
+            for half in halves:
                 for g in range(GROUPS):
                     sum_pass(unit, half, "arch", g)
 
-        def sum_all(unit):
-            sum_first(unit)
-            sum_arch(unit)
+        def sum_last(unit):
             for half in range(2):
                 sum_pass(unit, half, "live", 1)
 
-        def subtract_centres(unit):
-            for half in range(2):
+        def subtract_centres(unit, halves=(0, 1)):
+            for half in halves:
                 tile = flow.tile([P, BANK], BF16, name="v_rows", tag="v_rows", bufs=4)
                 nc.vector.scalar_tensor_tensor(
                     out=tile[:], in0=centres_sb[unit % 2][:, half * BANK : (half + 1) * BANK],
@@ -227,7 +238,7 @@ def tile_vlad_two_source_projection_k6_kernel(
                     cols = slice(g * P, (g + 1) * P)
                     nc.tensor.matmul_mx(
                         out=z[unit, half][:], lhsT=codes[:, cols].bitcast(FP8X4), lhsT_scale=scales[:, cols],
-                        rhs=w_codes[:].bitcast(FP8X4), rhs_scale=w_scales[:], start=g == 0, stop=g == GROUPS - 1,
+                        rhs=w_codes.bitcast(FP8X4), rhs_scale=w_scales, start=g == 0, stop=g == GROUPS - 1,
                     )
 
         def inverse_root(unit):
@@ -254,10 +265,18 @@ def tile_vlad_two_source_projection_k6_kernel(
                 )
             nc.sync.dma_start(out=y_out[unit * P : (unit + 1) * P, :], in_=y[unit][:])
 
-        def round_y(unit):
+        def round_y_on_vector(unit):
             for half in range(2):
                 y_rows[unit, half] = flow.tile([P, BANK], BF16, name="y_rows", tag="y_rows", bufs=4)
                 nc.vector.tensor_copy(out=y_rows[unit, half][:], in_=y[unit][:, half * BANK : (half + 1) * BANK])
+
+        def round_y(unit):
+            for half in range(2):
+                y_rows[unit, half] = flow.tile([P, BANK], BF16, name="y_rows", tag="y_rows", bufs=4)
+                nc.gpsimd.tensor_scalar(
+                    out=y_rows[unit, half][:], in0=y[unit][:, half * BANK : (half + 1) * BANK],
+                    scalar1=1.0, scalar2=0.0, op0=ALU.mult, op1=ALU.add,
+                )
 
         def turn_y(unit, tag="y_turned"):
             y_bank[unit] = psum.tile([P, BANK], F32, name=tag, tag=tag)
@@ -334,9 +353,6 @@ def tile_vlad_two_source_projection_k6_kernel(
 
             return rounded, exact, planes
 
-        def place_chunks(place):
-            return [("live", place), (place, 0, 0), (place, 0, 1), ("arch", place), (place, 1, 0), (place, 1, 1)]
-
         def feed(key, previous):
             copy_s(key)
             copy_v(key)
@@ -345,8 +361,7 @@ def tile_vlad_two_source_projection_k6_kernel(
 
         on_scalar, on_vector = nc.scalar.copy, nc.vector.tensor_copy
 
-        first = place_chunks(0)
-        stream = place_chunks(1) + place_chunks(2) + place_chunks(3)
+        first = [("live", 0, 0), (0, 0, 0), (0, 0, 1), ("arch", 0, 0), (0, 1, 0), (0, 1, 1)]
         w_chunks = [("w", g, half) for g in range(GROUPS) for half in range(2)]
         feed(first[0], None)
         feed(first[1], first[0])
@@ -361,7 +376,7 @@ def tile_vlad_two_source_projection_k6_kernel(
         sum_pass(0, 0, "live", 1)
         feed(w_chunks[0], first[5])
         sum_pass(0, 1, "live", 1)
-        sum_pass(1, 0, "live", 1)
+        sum_last(1)
         feed(w_chunks[1], w_chunks[0])
         sum_arch(0)
         quantise(w_chunks[1])
@@ -372,91 +387,94 @@ def tile_vlad_two_source_projection_k6_kernel(
         collect_v(0, on_scalar)
         feed(w_chunks[3], w_chunks[2])
         quantise_v(0)
-        feed(stream[0], w_chunks[3])
+        feed(("live", 1, 0), w_chunks[3])
         project(0)
-        feed(stream[1], stream[0])
-        feed(stream[2], stream[1])
-        pending = stream[2]
+        feed((1, 0, None), ("live", 1, 0))
 
         for unit in range(1, 6):
-            chunks = stream[3 * unit : 3 * unit + 3]
+            place, g = divmod(unit + 2, 2)
+            narrow, wide = (("live", "arch")[g], place, 0), (place, g, None)
+            pending = (*divmod(unit + 1, 2), None)
             back = unit - 2
             if unit % 2 == 1 and unit // 2 + 2 < PLACES:
                 load_place(unit // 2 + 2)
             if back >= 0:
                 inverse_root(back)
             quantise(pending)
-            sum_pass(unit, 1, "live", 1)
+            if unit > 1:
+                sum_last(unit)
             sum_first(unit + 1)
-            copy_v(chunks[0])
-            copy_s(chunks[0])
-            copy_v(chunks[1])
-            copy_s(chunks[1])
+            if back >= 0:
+                copy_v(narrow)
+            copy_s(narrow)
             if back > 0:
                 quantise_y(back - 1)
             if back >= 0:
                 power_law(back)
+                round_y(back)
                 project(back + 1)
             subtract_centres(unit)
             turn_v(unit)
             if back >= 0:
-                round_y(back)
                 turn_y(back)
-            quantise(chunks[0])
-            sum_arch(unit + 1)
-            copy_v(chunks[2])
-            copy_s(chunks[2])
+            else:
+                copy_v(narrow)
+            copy_s(wide)
+            if back >= 0:
+                quantise(narrow)
+                sum_arch(unit + 1)
+                copy_v(wide)
+            else:
+                copy_v(wide)
+                quantise(narrow)
+                sum_arch(unit + 1)
             collect_v(unit, on_scalar)
             if 0 <= back < 3:
                 collect_y(back, on_scalar)
-            quantise(chunks[1])
-            sum_pass(unit + 1, 0, "live", 1)
             quantise_v(unit)
-            pending = chunks[2]
 
-        inverse_root(4)
         sum_first(7)
-        quantise(pending)
-        sum_pass(6, 1, "live", 1)
         sum_arch(7)
+        inverse_root(4)
+        quantise((3, 1, None))
+        sum_last(6)
+        collect_y(3, on_scalar)
+        power_law(4)
+        round_y(4)
+        sum_last(7)
+        project(5)
         subtract_centres(6)
         turn_v(6)
-        sum_pass(7, 0, "live", 1)
-        sum_pass(7, 1, "live", 1)
-        collect_y(3, on_scalar)
-        collect_v(6, on_scalar)
-        power_law(4)
-        project(5)
         subtract_centres(7)
-        turn_v(7)
         inverse_root(5)
+        turn_y(4)
+        collect_v(6, on_vector)
+        turn_v(7)
+        quantise_y(3)
         quantise_v(6)
         project(6)
-        round_y(4)
-        turn_y(4)
-        quantise_y(3)
-        collect_v(7, on_scalar)
+        collect_y(4, on_scalar)
         power_law(5)
-        collect_y(4, on_vector)
-        inverse_root(6)
-        quantise_v(7)
-        project(7)
         round_y(5)
-        turn_y(5)
+        collect_v(7, on_vector)
+        inverse_root(6)
         quantise_y(4)
+        quantise_v(7)
+        turn_y(5)
+        project(7)
+        collect_y(5, on_vector)
         inverse_root(7)
         power_law(6)
-        round_y(6)
+        round_y_on_vector(6)
         turn_y(6, "v_turned")
-        collect_y(5, on_vector)
         rounded, exact, planes = finish_last(7)
+        quantise_y(5)
+        collect_y(6, on_scalar)
         rounded(0)
         rounded(1)
-        collect_y(6, on_scalar)
         exact(0)
-        exact(1)
-        quantise_y(5)
         quantise_y(6)
+        exact(1)
         planes(0)
         planes(1)
         store_words(3)

@@ -22,7 +22,9 @@ BANK = 512
 GROUPS = 2
 UNITS = 2 * PLACES
 VECTOR_NARROW = 248
-VECTOR_WIDE = 584
+VECTOR_HEAD = 584
+VECTOR_WIDE = 576
+VECTOR_LAST = 576
 EARLY_UNITS = 4
 
 
@@ -90,13 +92,13 @@ def tile_vlad_two_source_projection_k6_kernel(
         load_assignments(("arch", 0), a_arch[0], 1)
         load_rows(0, x_live[0], 1)
         nc.sync.dma_start(out=mass_rows[:], in_=mass.rearrange("i (h p) -> (i h) p", p=P))
-        load_arch_scales(0)
-        load_rows("w", w_proj, 0)
+        for g in range(GROUPS):
+            load_rows("w", w_proj, g)
         load_arch(0)
+        load_arch_scales(0)
         centres_sb = [keep.tile([P, WIDTH], BF16, name="centres_%d" % h) for h in range(2)]
-        nc.sync.dma_start(out=centres_sb[0][:], in_=centres[0:P, :])
-        load_rows("w", w_proj, 1)
-        nc.sync.dma_start(out=centres_sb[1][:], in_=centres[P : 2 * P, :])
+        for h in range(2):
+            nc.sync.dma_start(out=centres_sb[h][:], in_=centres[h * P : (h + 1) * P, :])
         load_place(1)
 
         mass_square = keep.tile([P, P], F32, name="mass_square")
@@ -110,7 +112,7 @@ def tile_vlad_two_source_projection_k6_kernel(
 
         nc.scalar.activation(out=mass_square[:], in_=ident[:], func=ACT.Abs_reciprocal_sqrt, bias=1.0)
 
-        grouped, quantised = {}, {}
+        grouped, quantised, shares = {}, {}, {}
 
         def interleave(engine_copy, dst, src):
             engine_copy(
@@ -129,7 +131,7 @@ def tile_vlad_two_source_projection_k6_kernel(
             if source in ("live", "arch"):
                 group = 0 if on_vector else 1
                 return dst[:, group * CLUSTERS : (group + 1) * CLUSTERS, :], raw_a[source, g][:, group]
-            split = VECTOR_NARROW if half is not None else VECTOR_WIDE
+            split = VECTOR_NARROW if half is not None else shares[key]
             cols = slice(0, split) if on_vector else slice(split, width)
             at = half * BANK if half is not None else 0
             return dst[:, cols, :], raw_x[source, g][:, :, at + cols.start : at + cols.stop]
@@ -361,120 +363,117 @@ def tile_vlad_two_source_projection_k6_kernel(
 
         on_scalar, on_vector = nc.scalar.copy, nc.vector.tensor_copy
 
-        first = [("live", 0, 0), (0, 0, 0), (0, 0, 1), ("arch", 0, 0), (0, 1, 0), (0, 1, 1)]
-        w_chunks = [("w", g, half) for g in range(GROUPS) for half in range(2)]
-        feed(first[0], None)
-        feed(first[1], first[0])
-        feed(first[2], first[1])
-        feed(first[3], first[2])
-        sum_first(0)
-        sum_first(1)
-        feed(first[4], first[3])
-        mass_bank = spread_mass()
-        feed(first[5], first[4])
-        nc.scalar.copy(out=minus_mass[:], in_=mass_bank[:, 0:UNITS])
-        sum_pass(0, 0, "live", 1)
-        feed(w_chunks[0], first[5])
-        sum_pass(0, 1, "live", 1)
-        sum_last(1)
-        feed(w_chunks[1], w_chunks[0])
+        head = [("live", 0, 0), (0, 0, 0), (0, 0, 1), ("arch", 0, 0), (0, 1, 0), (0, 1, 1)]
+        head.extend([("w", g, half) for g in range(GROUPS) for half in range(2)])
+        for k, key in enumerate(head):
+            feed(key, head[k - 1] if k > 0 else None)
+            if k > 0 and head[k - 1] == (0, 0, 1):
+                sum_first(0)
+                sum_first(1)
+                mass_bank = spread_mass()
+            if k > 0 and head[k - 1] == ("arch", 0, 0):
+                nc.scalar.copy(out=minus_mass[:], in_=mass_bank[:, 0:UNITS])
+            if k > 0 and head[k - 1] == (0, 1, 1):
+                sum_last(0)
+                sum_last(1)
         sum_arch(0)
-        quantise(w_chunks[1])
+        sum_arch(1)
+        quantise(head[-1])
         subtract_centres(0)
         turn_v(0)
-        sum_arch(1)
-        feed(w_chunks[2], None)
+        copy_s(("live", 1, 0))
         collect_v(0, on_scalar)
-        feed(w_chunks[3], w_chunks[2])
+        subtract_centres(1)
+        turn_v(1)
+        copy_v(("live", 1, 0))
         quantise_v(0)
-        feed(("live", 1, 0), w_chunks[3])
         project(0)
+        shares[1, 0, None] = VECTOR_HEAD
         feed((1, 0, None), ("live", 1, 0))
+        collect_v(1, on_scalar)
+        copy_v(("arch", 1, 0))
+        copy_s(("arch", 1, 0))
+        quantise((1, 0, None))
+        sum_first(2)
+        quantise_v(1)
+        shares[1, 1, None] = VECTOR_HEAD
+        load_place(2)
+        feed((1, 1, None), ("arch", 1, 0))
+        sum_arch(2)
 
-        for unit in range(1, 6):
+        for unit in range(2, 6):
             place, g = divmod(unit + 2, 2)
             narrow, wide = (("live", "arch")[g], place, 0), (place, g, None)
             pending = (*divmod(unit + 1, 2), None)
             back = unit - 2
-            if unit % 2 == 1 and unit // 2 + 2 < PLACES:
-                load_place(unit // 2 + 2)
-            if back >= 0:
-                inverse_root(back)
+            shares[wide] = VECTOR_LAST if unit == 5 else VECTOR_WIDE
+            if unit == 3:
+                load_place(3)
+            inverse_root(back)
             quantise(pending)
-            if unit > 1:
-                sum_last(unit)
+            sum_last(unit)
             sum_first(unit + 1)
-            if back >= 0:
-                copy_v(narrow)
+            copy_v(narrow)
             copy_s(narrow)
             if back > 0:
                 quantise_y(back - 1)
-            if back >= 0:
-                power_law(back)
-                round_y(back)
-                project(back + 1)
+            power_law(back)
+            round_y(back)
+            project(back + 1)
             subtract_centres(unit)
             turn_v(unit)
-            if back >= 0:
-                turn_y(back)
-            else:
-                copy_v(narrow)
+            turn_y(back)
             copy_s(wide)
-            if back >= 0:
-                quantise(narrow)
-                sum_arch(unit + 1)
-                copy_v(wide)
-            else:
-                copy_v(wide)
-                quantise(narrow)
-                sum_arch(unit + 1)
+            quantise(narrow)
+            sum_arch(unit + 1)
+            copy_v(wide)
             collect_v(unit, on_scalar)
-            if 0 <= back < 3:
+            if back < 3:
                 collect_y(back, on_scalar)
             quantise_v(unit)
 
         sum_first(7)
         sum_arch(7)
+        collect_y(3, on_scalar)
         inverse_root(4)
         quantise((3, 1, None))
         sum_last(6)
-        collect_y(3, on_scalar)
-        power_law(4)
-        round_y(4)
         sum_last(7)
-        project(5)
+        quantise_y(3)
         subtract_centres(6)
         turn_v(6)
+        power_law(4)
+        round_y(4)
+        project(5)
+        collect_v(6, on_scalar)
         subtract_centres(7)
         inverse_root(5)
-        turn_y(4)
-        collect_v(6, on_vector)
-        turn_v(7)
-        quantise_y(3)
         quantise_v(6)
+        turn_v(7)
         project(6)
-        collect_y(4, on_scalar)
+        turn_y(4)
+        collect_v(7, on_vector)
+        quantise_v(7)
+        project(7)
         power_law(5)
         round_y(5)
-        collect_v(7, on_vector)
+        collect_y(4, on_vector)
         inverse_root(6)
-        quantise_y(4)
-        quantise_v(7)
         turn_y(5)
-        project(7)
-        collect_y(5, on_vector)
         inverse_root(7)
         power_law(6)
-        round_y_on_vector(6)
+        round_y(6)
+        collect_y(5, on_vector)
+        quantise_y(4)
         turn_y(6, "v_turned")
         rounded, exact, planes = finish_last(7)
-        quantise_y(5)
-        collect_y(6, on_scalar)
         rounded(0)
         rounded(1)
+        collect_y(6, on_scalar)
+        quantise_y(5)
         exact(0)
-        quantise_y(6)
         exact(1)
+        quantise_y(6)
         planes(0)
         planes(1)
         store_words(3)

@@ -24,8 +24,8 @@ UNITS = 2 * PLACES
 VECTOR_NARROW = 248
 VECTOR_HEAD = 584
 VECTOR_WIDE = 576
-VECTOR_LAST = 576
-EARLY_UNITS = 4
+VECTOR_LAST = 264
+EARLY_PLACES = 2
 
 
 def tile_vlad_two_source_projection_k6_kernel(
@@ -131,7 +131,7 @@ def tile_vlad_two_source_projection_k6_kernel(
             if source in ("live", "arch"):
                 group = 0 if on_vector else 1
                 return dst[:, group * CLUSTERS : (group + 1) * CLUSTERS, :], raw_a[source, g][:, group]
-            split = VECTOR_NARROW if half is not None else shares[key]
+            split = shares.get(key, VECTOR_NARROW)
             cols = slice(0, split) if on_vector else slice(split, width)
             at = half * BANK if half is not None else 0
             return dst[:, cols, :], raw_x[source, g][:, :, at + cols.start : at + cols.stop]
@@ -216,14 +216,14 @@ def tile_vlad_two_source_projection_k6_kernel(
                 turn(v_bank[unit], v_rows[unit, g], g)
 
         def gather_words(engine_copy, dst, source):
-            engine_copy(
-                out=dst[:].bitcast(F32).rearrange("p (g c u) -> p g c u", g=GROUPS, u=2),
-                in_=source[:].rearrange("p (g u c) -> p g c u", g=GROUPS, u=2),
-            )
+            engine_copy(out=dst, in_=source[:].rearrange("p (g u c) -> p g c u", g=GROUPS, u=2))
+
+        def as_words(tile):
+            return tile[:].bitcast(F32).rearrange("p (g c u) -> p g c u", g=GROUPS, u=2)
 
         def collect_v(unit, engine_copy):
             v_cols[unit] = flow.tile([P, GROUPS * P * PACK], BF16, name="v_cols", tag="v_cols", align_bytes=64)
-            gather_words(engine_copy, v_cols[unit], v_bank[unit])
+            gather_words(engine_copy, as_words(v_cols[unit]), v_bank[unit])
 
         def quantise_v(unit):
             codes = flow.tile([P, GROUPS * P], U32, name="v_codes", tag="v_codes", align_bytes=64)
@@ -231,9 +231,9 @@ def tile_vlad_two_source_projection_k6_kernel(
             nc.vector.quantize_mx(out=codes[:].bitcast(FP8X4), scales=scales[:], in_=v_cols[unit][:])
             v_q[unit] = (codes, scales)
 
-        def project(unit):
+        def project(unit, halves=(0, 1)):
             codes, scales = v_q[unit]
-            for half in range(2):
+            for half in halves:
                 z[unit, half] = bank(2 if unit < UNITS - 2 else unit % 2, half)
                 for g in range(GROUPS):
                     w_codes, w_scales = quantised["w", g, half]
@@ -243,9 +243,11 @@ def tile_vlad_two_source_projection_k6_kernel(
                         rhs=w_codes.bitcast(FP8X4), rhs_scale=w_scales, start=g == 0, stop=g == GROUPS - 1,
                     )
 
-        def inverse_root(unit):
+        def inverse_root(unit, between=None):
             size = {}
             for half in range(2):
+                if half == 1 and between is not None:
+                    between()
                 size[half] = flow.tile([P, BANK], F32, name="size", tag="size", bufs=2)
                 nc.scalar.activation(out=size[half][:], in_=z[unit, half][:], func=ACT.Abs)
             for half in range(2):
@@ -286,11 +288,13 @@ def tile_vlad_two_source_projection_k6_kernel(
                 turn(y_bank[unit], y_rows[unit, g], g)
 
         def collect_y(unit, engine_copy):
-            y_cols[unit] = flow.tile([P, GROUPS * P * PACK], BF16, name="y_cols", tag="y_cols", align_bytes=64)
-            gather_words(engine_copy, y_cols[unit], y_bank[unit])
+            place, h = divmod(unit, 2)
+            if h == 0:
+                y_cols[place] = flow.tile([P, GROUPS * CLUSTERS * PACK], BF16, name="y_cols", tag="y_cols", align_bytes=64)
+            gather_words(engine_copy, as_words(y_cols[place])[:, :, h * P : (h + 1) * P, :], y_bank[unit])
 
-        early_scales = keep.tile([P, GROUPS, EARLY_UNITS * P], U8, name="early_scales", align_bytes=64)
-        late_scales = keep.tile([P, GROUPS, (UNITS - EARLY_UNITS) * P], U8, name="late_scales", align_bytes=64)
+        early_scales = keep.tile([P, GROUPS, EARLY_PLACES * CLUSTERS], U8, name="early_scales", align_bytes=64)
+        late_scales = keep.tile([P, GROUPS, (PLACES - EARLY_PLACES) * CLUSTERS], U8, name="late_scales", align_bytes=64)
         words_out = out_1.rearrange("g p m t -> p g (m t)").bitcast(I32)
 
         def store_scales(queues, plane, cols):
@@ -302,29 +306,27 @@ def tile_vlad_two_source_projection_k6_kernel(
 
         y_codes = {}
 
-        def store_words(place):
-            nc.sync.dma_start(
-                out=words_out[:, :, place * CLUSTERS : (place + 1) * CLUSTERS], in_=y_codes[place][:].bitcast(I32)
-            )
-
-        def quantise_y(unit):
-            place, h = divmod(unit, 2)
-            if h == 0:
+        def quantise_y_group(place, g):
+            plane, at = (early_scales, place) if place < EARLY_PLACES else (late_scales, place - EARLY_PLACES)
+            if g == 0:
                 y_codes[place] = flow.tile([P, GROUPS, CLUSTERS], U32, name="y_codes", tag="y_codes", align_bytes=64)
-            plane, at = (early_scales, unit * P) if unit < EARLY_UNITS else (late_scales, (unit - EARLY_UNITS) * P)
-            for g in range(GROUPS):
-                nc.vector.quantize_mx(
-                    out=y_codes[place][:, g, h * P : (h + 1) * P].bitcast(FP8X4), scales=plane[:, g, at : at + P],
-                    in_=y_cols[unit][:, g * BANK : (g + 1) * BANK],
+            nc.vector.quantize_mx(
+                out=y_codes[place][:, g, :].bitcast(FP8X4), scales=plane[:, g, at * CLUSTERS : (at + 1) * CLUSTERS],
+                in_=y_cols[place][:, g * CLUSTERS * PACK : (g + 1) * CLUSTERS * PACK],
+            )
+            if g == GROUPS - 1:
+                nc.sync.dma_start(
+                    out=words_out[:, :, place * CLUSTERS : (place + 1) * CLUSTERS], in_=y_codes[place][:].bitcast(I32)
                 )
-            if h == 1:
-                store_words(place)
-            if unit == EARLY_UNITS - 1:
-                store_scales([nc.sync], early_scales, slice(0, EARLY_UNITS * P))
+
+        def quantise_y(place):
+            for g in range(GROUPS):
+                quantise_y_group(place, g)
+            if place == EARLY_PLACES - 1:
+                store_scales([nc.sync], early_scales, slice(0, EARLY_PLACES * CLUSTERS))
 
         def finish_last(unit):
             y[unit] = flow.tile([P, PROJ], F32, name="y", tag="y", bufs=3)
-            at = (unit - EARLY_UNITS) * P
             turned = {}
 
             def rounded(half):
@@ -344,13 +346,9 @@ def tile_vlad_two_source_projection_k6_kernel(
                 nc.sync.dma_start(out=y_out[unit * P : (unit + 1) * P, window], in_=y[unit][:, window])
 
             def planes(half):
-                cols = flow.tile([P, P * PACK], BF16, name="last_cols", tag="last_cols", align_bytes=64)
                 nc.scalar.copy(
-                    out=cols[:].bitcast(F32).rearrange("p (c u) -> p c u", u=2),
+                    out=as_words(y_cols[unit // 2])[:, half, P : 2 * P, :],
                     in_=turned[half][:, 0 : 2 * P].rearrange("p (u c) -> p c u", u=2),
-                )
-                nc.vector.quantize_mx(
-                    out=y_codes[unit // 2][:, half, P : 2 * P].bitcast(FP8X4), scales=late_scales[:, half, at : at + P], in_=cols[:]
                 )
 
             return rounded, exact, planes
@@ -406,7 +404,7 @@ def tile_vlad_two_source_projection_k6_kernel(
             narrow, wide = (("live", "arch")[g], place, 0), (place, g, None)
             pending = (*divmod(unit + 1, 2), None)
             back = unit - 2
-            shares[wide] = VECTOR_LAST if unit == 5 else VECTOR_WIDE
+            shares[wide] = VECTOR_WIDE
             if unit == 3:
                 load_place(3)
             inverse_root(back)
@@ -415,43 +413,54 @@ def tile_vlad_two_source_projection_k6_kernel(
             sum_first(unit + 1)
             copy_v(narrow)
             copy_s(narrow)
-            if back > 0:
-                quantise_y(back - 1)
+            if back == 2:
+                quantise_y(0)
             power_law(back)
             round_y(back)
             project(back + 1)
             subtract_centres(unit)
             turn_v(unit)
             turn_y(back)
-            copy_s(wide)
-            quantise(narrow)
-            sum_arch(unit + 1)
-            copy_v(wide)
+            if unit == 5:
+                shares[3, 1, 0] = shares[3, 1, 1] = VECTOR_LAST
+                copy_s((3, 1, 0))
+                copy_s((3, 1, 1))
+                quantise(narrow)
+                sum_arch(6)
+                sum_first(7)
+                copy_v((3, 1, 0))
+                copy_v((3, 1, 1))
+                quantise((3, 1, 0))
+                sum_pass(6, 0, "live", 1)
+            else:
+                copy_s(wide)
+                quantise(narrow)
+                sum_arch(unit + 1)
+                copy_v(wide)
             collect_v(unit, on_scalar)
             if back < 3:
                 collect_y(back, on_scalar)
             quantise_v(unit)
 
-        sum_first(7)
-        sum_arch(7)
-        collect_y(3, on_scalar)
         inverse_root(4)
-        quantise((3, 1, None))
-        sum_last(6)
+        collect_y(3, on_scalar)
+        quantise((3, 1, 1))
+        sum_arch(7)
+        sum_pass(6, 1, "live", 1)
         sum_last(7)
-        quantise_y(3)
-        subtract_centres(6)
-        turn_v(6)
-        power_law(4)
+        subtract_centres(6, (0,))
+        power_law(4, lambda: subtract_centres(6, (1,)))
         round_y(4)
-        project(5)
-        collect_v(6, on_scalar)
+        project(5, (0,))
+        turn_v(6)
+        project(5, (1,))
         subtract_centres(7)
-        inverse_root(5)
+        inverse_root(5, lambda: collect_v(6, on_scalar))
         quantise_v(6)
         turn_v(7)
         project(6)
         turn_y(4)
+        quantise_y(1)
         collect_v(7, on_vector)
         quantise_v(7)
         project(7)
@@ -464,17 +473,15 @@ def tile_vlad_two_source_projection_k6_kernel(
         power_law(6)
         round_y(6)
         collect_y(5, on_vector)
-        quantise_y(4)
         turn_y(6, "v_turned")
         rounded, exact, planes = finish_last(7)
         rounded(0)
         rounded(1)
+        quantise_y(2)
         collect_y(6, on_scalar)
-        quantise_y(5)
-        exact(0)
-        exact(1)
-        quantise_y(6)
         planes(0)
         planes(1)
-        store_words(3)
-        store_scales([nc.scalar, nc.sync], late_scales, slice(EARLY_UNITS * P, UNITS * P))
+        exact(0)
+        exact(1)
+        quantise_y(3)
+        store_scales([nc.scalar, nc.sync], late_scales, slice(EARLY_PLACES * CLUSTERS, PLACES * CLUSTERS))

@@ -116,8 +116,8 @@ def tile_vlad_two_source_projection_k6_kernel(
 
         def interleave(engine_copy, dst, src):
             engine_copy(
-                out=dst.rearrange("p (c i) t -> p c t i", i=4),
-                in_=src.rearrange("p t (c i) -> p c t i", i=4),
+                out=dst.rearrange("p (c i) t -> p c t i", i=2),
+                in_=src.rearrange("p t (c i) -> p c t i", i=2),
             )
 
         def chunk_share(key, on_vector):

from contextlib import ExitStack

import concourse.mybir as mybir
from concourse.masks import make_identity

PLACES, CLUSTERS, DESCR, WIDTH, PROJ = 4, 256, 1024, 1024, 1024
FLOPS = 2 * PLACES * CLUSTERS * WIDTH * 2 * DESCR + 2 * PLACES * CLUSTERS * WIDTH * PROJ

F32 = mybir.dt.float32
BF16 = mybir.dt.bfloat16
U32 = mybir.dt.uint32
I32 = mybir.dt.int32
U8 = mybir.dt.uint8
FP8X4 = mybir.dt.float8_e4m3fn_x4
FP4X4 = mybir.dt.float4_e2m1fn_x4
ALU = mybir.AluOpType
ACT = mybir.ActivationFunctionType

P = 128
PACK = 4
BANK = 512
GROUPS = 2
UNITS = 2 * PLACES
VECTOR_NARROW = 248
VECTOR_HEAD = 584
VECTOR_WIDE = 576
VECTOR_LAST = 264
EARLY_PLACES = 2


def tile_vlad_two_source_projection_k6_kernel(
    tc, a_live, x_live, a_arch, arch_words, arch_scales, mass, centres, w_proj, out_0, out_1, out_2
):
    nc = tc.nc
    with ExitStack() as ctx:
        keep = ctx.enter_context(tc.tile_pool(name="keep", bufs=1))
        flow = ctx.enter_context(tc.tile_pool(name="flow", bufs=2))
        psum = ctx.enter_context(tc.psum_pool(name="psum", bufs=1))
        ctx.enter_context(tc.manual_schedule())

        ident = keep.tile([P, P], F32, name="ident")
        make_identity(nc, ident[:])
        arch_planes = []
        for place in range(PLACES):
            plane = keep.tile([P, GROUPS, WIDTH], U8, name="arch_plane_%d" % place, align_bytes=64)
            nc.vector.memset(plane[:].bitcast(I32), 0)
            arch_planes.append(plane)

        def load_arch_scales(place):
            cols = slice(place * WIDTH, (place + 1) * WIDTH)
            for quad in range(4):
                nc.sync.dma_start(
                    out=arch_planes[place][32 * quad : 32 * quad + 4, :, :].bitcast(I32),
                    in_=arch_scales[:, 4 * quad : 4 * quad + 4, cols].rearrange("g r n -> r g n").bitcast(I32),
                )

        raw_a, raw_x, arch = {}, {}, {}

        def load_assignments(key, source, pieces):
            tile = flow.tile([P, GROUPS, PACK, CLUSTERS], BF16, name="raw_a", tag="raw_a", bufs=4)
            rows = source.rearrange("(g p j) c -> p g j c", g=GROUPS, j=PACK)
            step = GROUPS // pieces
            for g in range(0, GROUPS, step):
                nc.sync.dma_start(out=tile[:, g : g + step], in_=rows[:, g : g + step])
            raw_a[key] = tile

        def load_rows(key, source, g, pieces=1):
            tile = flow.tile([P, PACK, WIDTH], BF16, name="raw_x", tag="raw_x", bufs=6)
            rows = source[g * BANK : (g + 1) * BANK, :].rearrange("(p j) d -> p j d", j=PACK)
            step = WIDTH // pieces
            for at in range(0, WIDTH, step):
                nc.sync.dma_start(out=tile[:, :, at : at + step], in_=rows[:, :, at : at + step])
            raw_x[key, g] = tile

        def load_arch(place):
            tile = flow.tile([P, GROUPS, 2 * WIDTH], U8, name="arch", tag="arch", bufs=PLACES, align_bytes=64)
            window = arch_words.rearrange("g p b -> p g b")[:, :, 2 * WIDTH * place : 2 * WIDTH * (place + 1)]
            nc.sync.dma_start(out=tile[:].bitcast(I32), in_=window.bitcast(I32))
            arch[place] = tile

        def load_place(place):
            load_assignments(("live", place), a_live[place], 1)
            load_rows(place, x_live[place], 0)
            load_assignments(("arch", place), a_arch[place], 1)
            load_rows(place, x_live[place], 1)
            load_arch(place)
            load_arch_scales(place)

        mass_rows = keep.tile([UNITS, P], BF16, name="mass_rows")
        load_assignments(("live", 0), a_live[0], 2)
        load_rows(0, x_live[0], 0, 2)
        load_assignments(("arch", 0), a_arch[0], 1)
        load_rows(0, x_live[0], 1)
        nc.sync.dma_start(out=mass_rows[:], in_=mass.rearrange("i (h p) -> (i h) p", p=P))
        for g in range(GROUPS):
            load_rows("w", w_proj, g)
        load_arch(0)
        load_arch_scales(0)
        centres_sb = [keep.tile([P, WIDTH], BF16, name="centres_%d" % h) for h in range(2)]
        for h in range(2):
            nc.sync.dma_start(out=centres_sb[h][:], in_=centres[h * P : (h + 1) * P, :])
        load_place(1)

        mass_square = keep.tile([P, P], F32, name="mass_square")
        minus_mass = keep.tile([P, UNITS], F32, name="minus_mass")

        def spread_mass():
            nc.scalar.activation(out=mass_square[0:UNITS, :], in_=mass_rows[:], func=ACT.Copy, scale=-1.0)
            mass_bank = psum.tile([P, BANK], F32, name="y_turned", tag="y_turned")
            nc.tensor.transpose(mass_bank[:, 0:P], mass_square[:], ident[:])
            return mass_bank

        nc.scalar.activation(out=mass_square[:], in_=ident[:], func=ACT.Abs_reciprocal_sqrt, bias=1.0)

        grouped, quantised, shares = {}, {}, {}

        def interleave(engine_copy, dst, src):
            engine_copy(
                out=dst.rearrange("p (c i) t -> p c t i", i=2),
                in_=src.rearrange("p t (c i) -> p c t i", i=2),
            )

        def chunk_share(key, on_vector):
            source, g, half = key
            width = BANK if half is not None else 2 * BANK
            if key not in grouped:
                grouped[key] = flow.tile(
                    [P, width * PACK], BF16, name="grouped", tag="grouped_%d" % width, bufs=3 if half is not None else 2, align_bytes=64
                )
            dst = grouped[key][:].rearrange("p (c t) -> p c t", t=PACK)
            if source in ("live", "arch"):
                group = 0 if on_vector else 1
                return dst[:, group * CLUSTERS : (group + 1) * CLUSTERS, :], raw_a[source, g][:, group]
            split = shares.get(key, VECTOR_NARROW)
            cols = slice(0, split) if on_vector else slice(split, width)
            at = half * BANK if half is not None else 0
            return dst[:, cols, :], raw_x[source, g][:, :, at + cols.start : at + cols.stop]

        def copy_v(key):
            interleave(nc.vector.tensor_copy, *chunk_share(key, True))

        def copy_s(key):
            interleave(nc.scalar.copy, *chunk_share(key, False))

        def quantise(key):
            source, g, half = key
            width = BANK if half is not None else 2 * BANK
            tag, bufs = ("w", 4) if source == "w" else ("op_%d" % width, 8 if half is not None else 4)
            codes = flow.tile([P, width], U32, name="codes", tag=tag + "_codes", bufs=bufs, align_bytes=64)
            scales = flow.tile([P, width], U8, name="scales", tag=tag + "_scales", bufs=bufs, align_bytes=64)
            nc.vector.quantize_mx(out=codes[:].bitcast(FP8X4), scales=scales[:], in_=grouped[key][:])
            if half is not None:
                quantised[key] = (codes[:], scales[:])
            else:
                for k in range(2):
                    cols = slice(k * BANK, (k + 1) * BANK)
                    quantised[source, g, k] = (codes[:, cols], scales[:, cols])

        sums, v_rows, v_bank, v_cols, v_q, z, root, y, y_rows, y_bank, y_cols = ({} for k in range(11))

        issued = {}

        def bank(pair, half):
            return psum.tile([P, BANK], F32, name="bank", tag="bank%d" % (2 * pair + half))

        def sum_pass(unit, half, source, g):
            place, h = divmod(unit, 2)
            issued[unit, half] = issued.get((unit, half), 0) + 1
            start, stop = issued[unit, half] == 1, issued[unit, half] == 2 * GROUPS
            if start:
                sums[unit, half] = bank(unit % 2, half)
            a_codes, a_scales = quantised[source, place, 0]
            cols = slice(g * CLUSTERS + h * P, g * CLUSTERS + (h + 1) * P)
            if source == "live":
                codes, scales = quantised[place, g, half]
                rhs, rhs_scale = codes.bitcast(FP8X4), scales
            else:
                rhs = arch[place][:, g, 2 * half * BANK : 2 * (half + 1) * BANK].bitcast(FP4X4)
                rhs_scale = arch_planes[place][:, g, half * BANK : (half + 1) * BANK]
            nc.tensor.matmul_mx(
                out=sums[unit, half][:], lhsT=a_codes[:, cols].bitcast(FP8X4), lhsT_scale=a_scales[:, cols],
                rhs=rhs, rhs_scale=rhs_scale, start=start, stop=stop,
            )

        def sum_first(unit):
            for half in range(2):
                sum_pass(unit, half, "live", 0)

        def sum_arch(unit, halves=(0, 1)):
            for half in halves:
                for g in range(GROUPS):
                    sum_pass(unit, half, "arch", g)

        def sum_last(unit):
            for half in range(2):
                sum_pass(unit, half, "live", 1)

        def subtract_centres(unit, halves=(0, 1)):
            for half in halves:
                tile = flow.tile([P, BANK], BF16, name="v_rows", tag="v_rows", bufs=4)
                nc.vector.scalar_tensor_tensor(
                    out=tile[:], in0=centres_sb[unit % 2][:, half * BANK : (half + 1) * BANK],
                    scalar=minus_mass[:, unit : unit + 1], in1=sums[unit, half][:], op0=ALU.mult, op1=ALU.add,
                )
                v_rows[unit, half] = tile

        def turn(target, rows, g):
            words = rows[:].bitcast(F32)
            for u in range(2):
                at = (2 * g + u) * P
                nc.tensor.transpose(target[:, at : at + P], words[:, u : 2 * P : 2], ident[:])

        def turn_v(unit, tag="v_turned"):
            v_bank[unit] = psum.tile([P, BANK], F32, name=tag, tag=tag)
            for g in range(GROUPS):
                turn(v_bank[unit], v_rows[unit, g], g)

        def gather_words(engine_copy, dst, source):
            engine_copy(out=dst, in_=source[:].rearrange("p (g u c) -> p g c u", g=GROUPS, u=2))

        def as_words(tile):
            return tile[:].bitcast(F32).rearrange("p (g c u) -> p g c u", g=GROUPS, u=2)

        def collect_v(unit, engine_copy):
            v_cols[unit] = flow.tile([P, GROUPS * P * PACK], BF16, name="v_cols", tag="v_cols", align_bytes=64)
            gather_words(engine_copy, as_words(v_cols[unit]), v_bank[unit])

        def quantise_v(unit):
            codes = flow.tile([P, GROUPS * P], U32, name="v_codes", tag="v_codes", align_bytes=64)
            scales = flow.tile([P, GROUPS * P], U8, name="v_scales", tag="v_scales", align_bytes=64)
            nc.vector.quantize_mx(out=codes[:].bitcast(FP8X4), scales=scales[:], in_=v_cols[unit][:])
            v_q[unit] = (codes, scales)

        def project(unit, halves=(0, 1)):
            codes, scales = v_q[unit]
            for half in halves:
                z[unit, half] = bank(2 if unit < UNITS - 2 else unit % 2, half)
                for g in range(GROUPS):
                    w_codes, w_scales = quantised["w", g, half]
                    cols = slice(g * P, (g + 1) * P)
                    nc.tensor.matmul_mx(
                        out=z[unit, half][:], lhsT=codes[:, cols].bitcast(FP8X4), lhsT_scale=scales[:, cols],
                        rhs=w_codes.bitcast(FP8X4), rhs_scale=w_scales, start=g == 0, stop=g == GROUPS - 1,
                    )

        def inverse_root(unit, between=None):
            size = {}
            for half in range(2):
                if half == 1 and between is not None:
                    between()
                size[half] = flow.tile([P, BANK], F32, name="size", tag="size", bufs=2)
                nc.scalar.activation(out=size[half][:], in_=z[unit, half][:], func=ACT.Abs)
            for half in range(2):
                root[unit, half] = flow.tile([P, BANK], F32, name="root", tag="root", bufs=4)
                nc.scalar.activation(
                    out=root[unit, half][:], in_=size[half][:], func=ACT.Abs_reciprocal_sqrt, bias=1.0
                )

        y_out = out_0.rearrange("i c f -> (i c) f")

        def power_law(unit, between=None):
            y[unit] = flow.tile([P, PROJ], F32, name="y", tag="y", bufs=3)
            for half in range(2):
                if half == 1 and between is not None:
                    between()
                nc.vector.tensor_tensor(
                    out=y[unit][:, half * BANK : (half + 1) * BANK], in0=z[unit, half][:],
                    in1=root[unit, half][:], op=ALU.mult,
                )
            nc.sync.dma_start(out=y_out[unit * P : (unit + 1) * P, :], in_=y[unit][:])

        def round_y_on_vector(unit):
            for half in range(2):
                y_rows[unit, half] = flow.tile([P, BANK], BF16, name="y_rows", tag="y_rows", bufs=4)
                nc.vector.tensor_copy(out=y_rows[unit, half][:], in_=y[unit][:, half * BANK : (half + 1) * BANK])

        def round_y(unit):
            for half in range(2):
                y_rows[unit, half] = flow.tile([P, BANK], BF16, name="y_rows", tag="y_rows", bufs=4)
                nc.gpsimd.tensor_scalar(
                    out=y_rows[unit, half][:], in0=y[unit][:, half * BANK : (half + 1) * BANK],
                    scalar1=1.0, scalar2=0.0, op0=ALU.mult, op1=ALU.add,
                )

        def turn_y(unit, tag="y_turned"):
            y_bank[unit] = psum.tile([P, BANK], F32, name=tag, tag=tag)
            for g in range(GROUPS):
                turn(y_bank[unit], y_rows[unit, g], g)

        def collect_y(unit, engine_copy):
            place, h = divmod(unit, 2)
            if h == 0:
                y_cols[place] = flow.tile([P, GROUPS * CLUSTERS * PACK], BF16, name="y_cols", tag="y_cols", align_bytes=64)
            gather_words(engine_copy, as_words(y_cols[place])[:, :, h * P : (h + 1) * P, :], y_bank[unit])

        early_scales = keep.tile([P, GROUPS, EARLY_PLACES * CLUSTERS], U8, name="early_scales", align_bytes=64)
        late_scales = keep.tile([P, GROUPS, (PLACES - EARLY_PLACES) * CLUSTERS], U8, name="late_scales", align_bytes=64)
        words_out = out_1.rearrange("g p m t -> p g (m t)").bitcast(I32)

        def store_scales(queues, plane, cols):
            for quad in range(4):
                queues[quad % len(queues)].dma_start(
                    out=out_2[:, 4 * quad : 4 * quad + 4, cols].rearrange("g r m -> r g m").bitcast(I32),
                    in_=plane[32 * quad : 32 * quad + 4, :, :].bitcast(I32),
                )

        y_codes = {}

        def quantise_y_group(place, g):
            plane, at = (early_scales, place) if place < EARLY_PLACES else (late_scales, place - EARLY_PLACES)
            if g == 0:
                y_codes[place] = flow.tile([P, GROUPS, CLUSTERS], U32, name="y_codes", tag="y_codes", align_bytes=64)
            nc.vector.quantize_mx(
                out=y_codes[place][:, g, :].bitcast(FP8X4), scales=plane[:, g, at * CLUSTERS : (at + 1) * CLUSTERS],
                in_=y_cols[place][:, g * CLUSTERS * PACK : (g + 1) * CLUSTERS * PACK],
            )
            if g == GROUPS - 1:
                nc.sync.dma_start(
                    out=words_out[:, :, place * CLUSTERS : (place + 1) * CLUSTERS], in_=y_codes[place][:].bitcast(I32)
                )

        def quantise_y(place):
            for g in range(GROUPS):
                quantise_y_group(place, g)
            if place == EARLY_PLACES - 1:
                store_scales([nc.sync], early_scales, slice(0, EARLY_PLACES * CLUSTERS))

        def finish_last(unit):
            y[unit] = flow.tile([P, PROJ], F32, name="y", tag="y", bufs=3)
            turned = {}

            def rounded(half):
                y_rows[unit, half] = flow.tile([P, BANK], BF16, name="y_rows", tag="y_rows", bufs=4)
                nc.vector.tensor_tensor(
                    out=y_rows[unit, half][:], in0=z[unit, half][:], in1=root[unit, half][:], op=ALU.mult
                )
                tag = "bank%d" % (4 + half)
                turned[half] = psum.tile([P, BANK], F32, name=tag, tag=tag)
                turn(turned[half], y_rows[unit, half], 0)

            def exact(half):
                window = slice(half * BANK, (half + 1) * BANK)
                nc.vector.tensor_tensor(
                    out=y[unit][:, window], in0=z[unit, half][:], in1=root[unit, half][:], op=ALU.mult
                )
                nc.sync.dma_start(out=y_out[unit * P : (unit + 1) * P, window], in_=y[unit][:, window])

            def planes(half):
                nc.scalar.copy(
                    out=as_words(y_cols[unit // 2])[:, half, P : 2 * P, :],
                    in_=turned[half][:, 0 : 2 * P].rearrange("p (u c) -> p c u", u=2),
                )

            return rounded, exact, planes

        def feed(key, previous):
            copy_s(key)
            copy_v(key)
            if previous is not None:
                quantise(previous)

        on_scalar, on_vector = nc.scalar.copy, nc.vector.tensor_copy

        head = [("live", 0, 0), (0, 0, 0), (0, 0, 1), ("arch", 0, 0), (0, 1, 0), (0, 1, 1)]
        head.extend([("w", g, half) for g in range(GROUPS) for half in range(2)])
        for k, key in enumerate(head):
            feed(key, head[k - 1] if k > 0 else None)
            if k > 0 and head[k - 1] == (0, 0, 1):
                sum_first(0)
                sum_first(1)
                mass_bank = spread_mass()
            if k > 0 and head[k - 1] == ("arch", 0, 0):
                nc.scalar.copy(out=minus_mass[:], in_=mass_bank[:, 0:UNITS])
            if k > 0 and head[k - 1] == (0, 1, 1):
                sum_last(0)
                sum_last(1)
        sum_arch(0)
        sum_arch(1)
        quantise(head[-1])
        subtract_centres(0)
        turn_v(0)
        copy_s(("live", 1, 0))
        collect_v(0, on_scalar)
        subtract_centres(1)
        turn_v(1)
        copy_v(("live", 1, 0))
        quantise_v(0)
        project(0)
        shares[1, 0, None] = VECTOR_HEAD
        feed((1, 0, None), ("live", 1, 0))
        collect_v(1, on_scalar)
        copy_v(("arch", 1, 0))
        copy_s(("arch", 1, 0))
        quantise((1, 0, None))
        sum_first(2)
        quantise_v(1)
        shares[1, 1, None] = VECTOR_HEAD
        load_place(2)
        feed((1, 1, None), ("arch", 1, 0))
        sum_arch(2)

        for unit in range(2, 6):
            place, g = divmod(unit + 2, 2)
            narrow, wide = (("live", "arch")[g], place, 0), (place, g, None)
            pending = (*divmod(unit + 1, 2), None)
            back = unit - 2
            shares[wide] = VECTOR_WIDE
            if unit == 3:
                load_place(3)
            inverse_root(back)
            quantise(pending)
            sum_last(unit)
            sum_first(unit + 1)
            copy_v(narrow)
            copy_s(narrow)
            if back == 2:
                quantise_y(0)
            power_law(back)
            round_y(back)
            project(back + 1)
            subtract_centres(unit)
            turn_v(unit)
            turn_y(back)
            if unit == 5:
                shares[3, 1, 0] = shares[3, 1, 1] = VECTOR_LAST
                copy_s((3, 1, 0))
                copy_s((3, 1, 1))
                quantise(narrow)
                sum_arch(6)
                sum_first(7)
                copy_v((3, 1, 0))
                copy_v((3, 1, 1))
                quantise((3, 1, 0))
                sum_pass(6, 0, "live", 1)
            else:
                copy_s(wide)
                quantise(narrow)
                sum_arch(unit + 1)
                copy_v(wide)
            collect_v(unit, on_scalar)
            if back < 3:
                collect_y(back, on_scalar)
            quantise_v(unit)

        inverse_root(4)
        collect_y(3, on_scalar)
        quantise((3, 1, 1))
        sum_arch(7)
        sum_pass(6, 1, "live", 1)
        sum_last(7)
        subtract_centres(6, (0,))
        power_law(4, lambda: subtract_centres(6, (1,)))
        round_y(4)
        project(5, (0,))
        turn_v(6)
        project(5, (1,))
        subtract_centres(7)
        inverse_root(5, lambda: collect_v(6, on_scalar))
        quantise_v(6)
        turn_v(7)
        project(6)
        turn_y(4)
        quantise_y(1)
        collect_v(7, on_vector)
        quantise_v(7)
        project(7)
        power_law(5)
        round_y(5)
        collect_y(4, on_vector)
        inverse_root(6)
        turn_y(5)
        inverse_root(7)
        power_law(6)
        round_y(6)
        collect_y(5, on_vector)
        turn_y(6, "v_turned")
        rounded, exact, planes = finish_last(7)
        rounded(0)
        rounded(1)
        quantise_y(2)
        collect_y(6, on_scalar)
        planes(0)
        planes(1)
        exact(0)
        exact(1)
        quantise_y(3)
        store_scales([nc.scalar, nc.sync], late_scales, slice(EARLY_PLACES * CLUSTERS, PLACES * CLUSTERS))
